import numpy as np
import ml_dtypes


def mxq(x, axis, fmt="e4m3"):
    dtype, down = {"e4m3": (ml_dtypes.float8_e4m3fn, 7), "e5m2": (ml_dtypes.float8_e5m2, 14)}[fmt]
    v = np.moveaxis(np.asarray(x, np.float32).astype(ml_dtypes.bfloat16).astype(np.float64), axis, -1)
    blocks = v.reshape(v.shape[:-1] + (-1, 32))
    amax = np.abs(blocks).max(-1, keepdims=True)
    byte = np.maximum(np.where(amax > 0, np.frexp(amax)[1] - 1 + 127, 0) - down, 1)
    scale = np.exp2(byte - 127.0)
    codes = (blocks / scale).astype(np.float32).astype(dtype).astype(np.float64)
    return np.moveaxis((codes * scale).reshape(v.shape), -1, axis)


WIDE = False


def mx_kscale(k):
    if not WIDE:
        return np.ones(k)
    levels = np.array([30, -30])
    if k % 512:
        return np.exp2(np.random.permutation(np.resize(levels, k // 32))).repeat(32)
    a = np.empty((k // 512, 16))
    for p in range(k // 512):
        a[p, :8] = np.random.permutation(np.resize(levels, 8))
        for g in range(8):
            far = levels[np.abs(levels - a[p, g]) >= 10]
            a[p, g + 8] = far[np.random.randint(len(far))]
    return np.exp2(a.ravel()).repeat(32)


def f64(x):
    return np.asarray(x).astype(np.float64)


def striped(idx):
    return np.tile(np.asarray(idx).reshape(-1, 16).T, (8, 1)).astype(np.uint16)


def unstriped(offs):
    return offs[:16].T.reshape(-1).astype(np.int64)


E2M1 = np.array([0.0, 0.5, 1.0, 1.5, 2.0, 3.0, 4.0, 6.0, -0.0, -0.5, -1.0, -1.5, -2.0, -3.0, -4.0, -6.0])


def pack_weight(w, fmt):
    k, n = w.shape
    w = f64(np.asarray(w, np.float32).astype(ml_dtypes.bfloat16)).reshape(k // 32, 32, n)
    amax = np.abs(w).max(1)
    if fmt == "e4m3":
        byte = np.frexp(amax)[1] - 1 + 127 - 7
    else:
        mant, ex = np.frexp(amax / 6.0)
        byte = np.where(mant > 0.5, ex, ex - 1) + 127
    byte = np.clip(np.where(amax > 0, byte, 1), 1, 254)
    scaled = (w * np.exp2(127.0 - byte)[:, None, :]).reshape(k, n).astype(np.float32)
    by_word = np.ascontiguousarray(scaled.reshape(k // 512, 128, 4, n).transpose(0, 1, 3, 2))
    if fmt == "e4m3":
        words = by_word.astype(ml_dtypes.float8_e4m3fn).view(np.uint8)
    else:
        c = by_word.astype(ml_dtypes.float4_e2m1fn).view(np.uint8) & 0xF
        words = (c[..., 0::2] | (c[..., 1::2] << 4)).reshape(k // 512, 128, 2 * n)
    return np.ascontiguousarray(words), np.ascontiguousarray(byte.astype(np.uint8).reshape(k // 512, 16, n))


def unpack_weight(words, scales, fmt):
    g, _, n = scales.shape
    words = np.ascontiguousarray(words).reshape(g, 128, n, -1)
    if fmt == "e4m3":
        vals = words.view(ml_dtypes.float8_e4m3fn).astype(np.float64)
    else:
        nib = np.empty((g, 128, n, 4), np.uint8)
        nib[..., 0::2] = words & 0xF
        nib[..., 1::2] = words >> 4
        vals = E2M1[nib]
    vals = vals * np.repeat(np.exp2(scales.astype(np.float64) - 127.0), 8, axis=1)[..., None]
    return vals.transpose(0, 1, 3, 2).reshape(g * 512, n)


K, T, J, R, F, Z, O, N, E = 512, 1024, 256, 512, 512, 1024, 128, 256, 1024


def setup_inputs():
    n = np.random.standard_normal
    idx = np.random.permutation(T)[:J]
    idx2 = np.random.permutation(Z)[:J]
    idx3 = np.random.permutation(J)[:O]
    idx4 = np.random.permutation(J)[:O]
    idx5 = np.random.permutation(E)[:O]
    fk = mx_kscale(K)
    fr = mx_kscale(R)
    ff = mx_kscale(F)
    wp = pack_weight(n((K, R)) * 1 / np.sqrt(K) / fk[:, None] * fr, "e4m3")
    xop = pack_weight(n((F, Z)) / ff[:, None], "e4m3")
    w2p = pack_weight(n((F, R)) * 1 / np.sqrt(F) * ff[:, None] * fr, "e2m1")
    wbp = pack_weight(n((R, N)) * 1 / np.sqrt(R) / fr[:, None], "e2m1")
    return {
        "cq": (np.random.randint(-7, 8, (K, T)).astype(np.float64)).astype(np.float32),
        "ga": (np.random.uniform(0.1, 0.4, (K, 1)) * fk[:, None]).astype(np.float32),
        "w_words": wp[0],
        "w_scales": wp[1],
        "xo_words": xop[0],
        "xo_scales": xop[1],
        "w2_words": w2p[0],
        "w2_scales": w2p[1],
        "sa": (np.random.uniform(0.5, 1.6, (R, 1))).astype(np.float32),
        "sb": (np.random.uniform(0.5, 1.6, (R, 1))).astype(np.float32),
        "wb_words": wbp[0],
        "wb_scales": wbp[1],
        "tz": (np.random.randint(-9, 10, (N, E)).astype(np.float64)).astype(np.float32),
        "so": (np.random.uniform(0.1, 0.3, (N, 1))).astype(np.float32),
        "offs": striped(idx),
        "offs2": striped(idx2),
        "offs3": striped(idx3),
        "offs4": striped(idx4),
        "offs5": striped(idx5),
    }


def reference(cq, ga, w_words, w_scales, xo_words, xo_scales, w2_words, w2_scales, sa, sb, wb_words, wb_scales, tz, so, offs, offs2, offs3, offs4, offs5):
    idx = unstriped(offs)
    idx2 = unstriped(offs2)
    idx3 = unstriped(offs3)
    idx4 = unstriped(offs4)
    idx5 = unstriped(offs5)
    wu = unpack_weight(w_words, w_scales, "e4m3")
    xou = unpack_weight(xo_words, xo_scales, "e4m3")
    w2u = unpack_weight(w2_words, w2_scales, "e2m1")
    wbu = unpack_weight(wb_words, wb_scales, "e2m1")
    x1 = f64(cq)[:, idx] * f64(ga)
    x1q = mxq(x1, 0, "e4m3")
    a = wu.T @ x1q
    xoidx2g = xou[:, idx2]
    b = w2u.T @ xoidx2g
    hid = np.maximum(a[:, idx3] * f64(sa), b[:, idx4] * f64(sb))
    hidq = mxq(hid, 0, "e5m2")
    p = wbu.T @ hidq
    y = np.maximum(p, f64(tz)[:, idx5] * f64(so))
    return y

@@ -1,0 +1,197 @@
+from contextlib import ExitStack
+
+import concourse.mybir as mybir
+
+K, T, J, R, F, Z, O, N, E = 512, 1024, 256, 512, 512, 1024, 128, 256, 1024
+FLOPS = 2 * (K * R * J + F * R * J + R * N * O)
+
+F32 = mybir.dt.float32
+BF16 = mybir.dt.bfloat16
+I32 = mybir.dt.int32
+U32 = mybir.dt.uint32
+U16 = mybir.dt.uint16
+U8 = mybir.dt.uint8
+E4M3 = mybir.dt.float8_e4m3fn_x4
+E5M2 = mybir.dt.float8_e5m2_x4
+E2M1 = mybir.dt.float4_e2m1fn_x4
+COPY = mybir.ActivationFunctionType.Copy
+MAX = mybir.AluOpType.max
+
+P = 128
+PACK = 4
+QUAD = 32
+QUADS = P // QUAD
+LINE = 4
+
+
+def tile_list_weighedboth_codednote_one_stepfloor_kernel(
+    tc, cq, ga, w_words, w_scales, xo_words, xo_scales, w2_words, w2_scales, sa, sb,
+    wb_words, wb_scales, tz, so, offs, offs2, offs3, offs4, offs5, out,
+):
+    nc = tc.nc
+    with ExitStack() as ctx:
+        sb_pool = ctx.enter_context(tc.tile_pool(name="keep", bufs=1))
+        psum = ctx.enter_context(tc.psum_pool(name="psum", bufs=1))
+
+        def sbuf(name, shape, dtype):
+            return sb_pool.tile(shape, dtype, name=name, align_bytes=64)
+
+        lists = {}
+
+        def load_list(name, dram):
+            lists[name] = sb_pool.tile(list(dram.shape), U16, name=name)
+            nc.sync.dma_start(lists[name][:], dram)
+
+        def staged_rows(scales):
+            return scales[0].bitcast(I32).rearrange("(q r) c -> r q c", r=PACK)
+
+        xo_w = sbuf("xo_w", [P, Z], U32)
+        xo_stage = sbuf("xo_stage", [PACK, QUADS, Z // 4], I32)
+        xo_s = sbuf("xo_s", [P, Z], U8)
+        w2_raw = sbuf("w2_raw", [P, 2 * R], U8)
+        w2_stage = sbuf("w2_stage", [PACK, QUADS, R // 4], I32)
+        w_raw = sbuf("w_raw", [P, R], U32)
+        w_stage = sbuf("w_stage", [PACK, QUADS, R // 4], I32)
+        wb_w = sbuf("wb_w", [P, 2 * N], U8)
+        wb_stage = sbuf("wb_stage", [PACK, QUADS, N // 4], I32)
+        wb_s = sbuf("wb_s", [P, N], U8)
+        cq_t = [sbuf(f"cq{t}", [P, T], F32) for t in range(PACK)]
+        tz_t = [sbuf(f"tz{s}", [P, E], F32) for s in range(N // P)]
+        ga_sb = sbuf("ga_sb", [P, PACK], F32)
+        sa_sb = sbuf("sa_sb", [P, PACK], F32)
+        sb_sb = sbuf("sb_sb", [P, PACK], F32)
+        so_sb = sbuf("so_sb", [P, N // P], F32)
+
+        w2_nat = sbuf("w2_nat", [P, R], U8)
+        w_nat = sbuf("w_nat", [P, R], U8)
+        nc.vector.memset(xo_s[:].bitcast(I32), 0)
+        nc.vector.memset(w2_nat[:].bitcast(I32), 0)
+        nc.vector.memset(w_nat[:].bitcast(I32), 0)
+        nc.vector.memset(wb_s[:].bitcast(I32), 0)
+
+        cq_rows = cq.rearrange("(p t) c -> t p c", t=PACK)
+        nc.scalar.dma_start(xo_stage[:], staged_rows(xo_scales))
+        nc.scalar.dma_start(w2_stage[:], staged_rows(w2_scales))
+        nc.sync.dma_start(xo_w[:].bitcast(I32), xo_words[0].rearrange("p n t -> p (n t)").bitcast(I32))
+        load_list("offs2", offs2)
+        nc.sync.dma_start(w2_raw[:].bitcast(I32), w2_words[0].bitcast(I32))
+        load_list("offs", offs)
+        nc.sync.dma_start(cq_t[0][:], cq_rows[0])
+        nc.sync.dma_start(cq_t[1][:], cq_rows[1])
+        load_list("offs4", offs4)
+        nc.sync.dma_start(w_stage[:], staged_rows(w_scales))
+        for t in range(2, PACK):
+            nc.sync.dma_start(cq_t[t][:], cq_rows[t])
+        nc.sync.dma_start(w_raw[:].bitcast(I32), w_words[0].rearrange("p n t -> p (n t)").bitcast(I32))
+        load_list("offs3", offs3)
+        nc.sync.dma_start(wb_w[:].bitcast(I32), wb_words[0].bitcast(I32))
+        load_list("offs5", offs5)
+        for s in range(N // P):
+            nc.sync.dma_start(tz_t[s][:], tz[s * P:(s + 1) * P, :])
+
+        nc.gpsimd.dma_start(ga_sb[:], ga.rearrange("(p t) o -> p (t o)", t=PACK))
+        nc.gpsimd.dma_start(sb_sb[:], sb.rearrange("(p t) o -> p (t o)", t=PACK))
+        nc.gpsimd.dma_start(sa_sb[:], sa.rearrange("(p t) o -> p (t o)", t=PACK))
+        with nc.allow_non_contiguous_dma(reason="two steps a partition"):
+            nc.gpsimd.dma_start(so_sb[:], so.rearrange("(s p) o -> p (s o)", p=P))
+        nc.gpsimd.dma_start(wb_stage[:], staged_rows(wb_scales))
+
+        def spread_low(plane, stage):
+            for q in range(QUADS):
+                nc.vector.tensor_copy(plane[:].bitcast(I32)[QUAD * q:QUAD * q + PACK, :], stage[:, q, :])
+
+        def dealt_out(ap):
+            return ap.rearrange("p t (c i) -> p c t i", i=LINE)
+
+        def dealt_in(ap):
+            return ap.rearrange("p (c i t) -> p c t i", i=LINE, t=PACK)
+
+        def woven_out(ap):
+            return ap.rearrange("p (c i) t -> p c t i", i=LINE)
+
+        def woven_in(ap):
+            return ap.rearrange("p t (c i) -> p c t i", i=LINE)
+
+        banks = {}
+
+        def bank(idx, width, name):
+            banks[name] = psum.tile([P, width], F32, name=name, tag=f"bank{idx}")
+            return banks[name]
+
+        spread_low(xo_s, xo_stage)
+        xg_s = sbuf("xg_s", [P, J], U8)
+        nc.vector.tensor_copy(xg_s[:], xo_s[:].indirect(lists["offs2"][:]))
+        xg_w = sbuf("xg_w", [P, J], U32)
+        nc.vector.tensor_copy(xg_w[:], xo_w[:].indirect(lists["offs2"][:]))
+        spread_low(w2_nat, w2_stage)
+        w2_s = sbuf("w2_s", [P, PACK, P], U8)
+        nc.vector.tensor_copy(w2_s[:], w2_nat[:].rearrange("p (m t) -> p t m", t=PACK))
+        w2_w = sbuf("w2_w", [P, PACK, 2 * P], U8)
+        nc.scalar.copy(dealt_out(w2_w[:].bitcast(U16)), dealt_in(w2_raw[:].bitcast(U16)))
+
+        x1 = sbuf("x1", [P, PACK, J], BF16)
+
+        def fetch_codes(t):
+            nc.scalar.activation(x1[:, t, :], cq_t[t][:].indirect(lists["offs"][:]), COPY, scale=ga_sb[:, t:t + 1])
+
+        b_t = [sbuf(f"b{t}", [P, J], F32) for t in range(PACK)]
+        gb = sbuf("gb", [P, PACK, O], F32)
+        for t in range(PACK):
+            acc = bank(t, J, f"bacc{t}")
+            nc.tensor.matmul_mx(acc[:], lhsT=w2_w[:, t, :].bitcast(E2M1), lhsT_scale=w2_s[:, t, :],
+                                rhs=xg_w[:].bitcast(E4M3), rhs_scale=xg_s[:], start=True, stop=True)
+            nc.vector.tensor_copy(b_t[t][:], acc[:])
+
+        spread_low(w_nat, w_stage)
+        w_s = sbuf("w_s", [P, PACK, P], U8)
+        nc.vector.tensor_copy(w_s[:], w_nat[:].rearrange("p (m t) -> p t m", t=PACK))
+        spread_low(wb_s, wb_stage)
+
+        def fetch_b(t):
+            nc.scalar.activation(gb[:, t, :], b_t[t][:].indirect(lists["offs4"][:]), COPY, scale=sb_sb[:, t:t + 1])
+
+        fetch_codes(0)
+        fetch_codes(1)
+        fetch_b(0)
+        fetch_b(1)
+        fetch_codes(2)
+        fetch_b(2)
+        fetch_b(3)
+        fetch_codes(3)
+
+        w_w = sbuf("w_w", [P, PACK, P], U32)
+        nc.scalar.copy(dealt_out(w_w[:]), dealt_in(w_raw[:]))
+        x1i = sbuf("x1i", [P, J, PACK], BF16)
+        xq_w = sbuf("xq_w", [P, J], U32)
+        xq_s = sbuf("xq_s", [P, J], U8)
+        halves = [slice(0, J // 2), slice(J // 2, J)]
+        for h in halves:
+            nc.vector.tensor_copy(woven_out(x1i[:, h, :]), woven_in(x1[:, :, h]))
+        for h in halves:
+            nc.vector.quantize_mx(out=xq_w[:, h].bitcast(E4M3), scales=xq_s[:, h],
+                                  in_=x1i[:, h, :].rearrange("p j t -> p (j t)"))
+        a_t = [sbuf(f"a{t}", [P, J], F32) for t in range(PACK)]
+        g_a = sbuf("g_a", [P, PACK, O], F32)
+        for t in range(PACK):
+            acc = bank(PACK + t, J, f"aacc{t}")
+            nc.tensor.matmul_mx(acc[:], lhsT=w_w[:, t, :].bitcast(E4M3), lhsT_scale=w_s[:, t, :],
+                                rhs=xq_w[:].bitcast(E4M3), rhs_scale=xq_s[:], start=True, stop=True)
+            nc.vector.tensor_copy(a_t[t][:], acc[:])
+            nc.scalar.activation(g_a[:, t, :], a_t[t][:].indirect(lists["offs3"][:]), COPY, scale=sa_sb[:, t:t + 1])
+
+        hid = sbuf("hid", [P, O, PACK], BF16)
+        nc.vector.tensor_tensor(woven_out(hid[:]), woven_in(g_a[:]), woven_in(gb[:]), MAX)
+        hq_w = sbuf("hq_w", [P, O], U32)
+        hq_s = sbuf("hq_s", [P, O], U8)
+        nc.vector.quantize_mx(out=hq_w[:].bitcast(E5M2), scales=hq_s[:], in_=hid[:].rearrange("p o t -> p (o t)"))
+        queues = [nc.sync, nc.scalar]
+        for s in range(N // P):
+            floor = sbuf(f"floor{s}", [P, O], F32)
+            nc.scalar.activation(floor[:], tz_t[s][:].indirect(lists["offs5"][:]), COPY, scale=so_sb[:, s:s + 1])
+            acc = bank(s, O, f"pacc{s}")
+            nc.tensor.matmul_mx(acc[:], lhsT=wb_w[:, 2 * P * s:2 * P * (s + 1)].bitcast(E2M1),
+                                lhsT_scale=wb_s[:, P * s:P * (s + 1)],
+                                rhs=hq_w[:].bitcast(E5M2), rhs_scale=hq_s[:], start=True, stop=True)
+            y = sbuf(f"y{s}", [P, O], F32)
+            nc.vector.tensor_tensor(y[:], acc[:], floor[:], MAX)
+            queues[s].dma_start(out[s * P:(s + 1) * P, :], y[:])

@@ -33,8 +33,8 @@ def tile_list_weighedboth_codednote_one_stepfloor_kernel(
         sb_pool = ctx.enter_context(tc.tile_pool(name="keep", bufs=1))
         psum = ctx.enter_context(tc.psum_pool(name="psum", bufs=1))
 
-        def sbuf(name, shape, dtype):
-            return sb_pool.tile(shape, dtype, name=name, align_bytes=64)
+        def sbuf(name, shape, dtype, tag=None):
+            return sb_pool.tile(shape, dtype, name=name, tag=tag or name, align_bytes=64)
 
         lists = {}
 
@@ -45,13 +45,19 @@ def tile_list_weighedboth_codednote_one_stepfloor_kernel(
         def staged_rows(scales):
             return scales[0].bitcast(I32).rearrange("(q r) c -> r q c", r=PACK)
 
+        def per_row(v):
+            return v.rearrange("(p t) o -> p (t o)", t=PACK)
+
+        def words(v):
+            return v[0].rearrange("p n t -> p (n t)").bitcast(I32)
+
         xo_w = sbuf("xo_w", [P, Z], U32)
         xo_stage = sbuf("xo_stage", [PACK, QUADS, Z // 4], I32)
         xo_s = sbuf("xo_s", [P, Z], U8)
         w2_raw = sbuf("w2_raw", [P, 2 * R], U8)
-        w2_stage = sbuf("w2_stage", [PACK, QUADS, R // 4], I32)
         w_raw = sbuf("w_raw", [P, R], U32)
-        w_stage = sbuf("w_stage", [PACK, QUADS, R // 4], I32)
+        ww_stage = sbuf("ww_stage", [PACK, 2, QUADS, R // 4], I32)
+        ww_nat = sbuf("ww_nat", [P, 2 * R], U8)
         wb_w = sbuf("wb_w", [P, 2 * N], U8)
         wb_stage = sbuf("wb_stage", [PACK, QUADS, N // 4], I32)
         wb_s = sbuf("wb_s", [P, N], U8)
@@ -62,39 +68,35 @@ def tile_list_weighedboth_codednote_one_stepfloor_kernel(
         sb_sb = sbuf("sb_sb", [P, PACK], F32)
         so_sb = sbuf("so_sb", [P, N // P], F32)
 
-        w2_nat = sbuf("w2_nat", [P, R], U8)
-        w_nat = sbuf("w_nat", [P, R], U8)
         nc.vector.memset(xo_s[:].bitcast(I32), 0)
-        nc.vector.memset(w2_nat[:].bitcast(I32), 0)
-        nc.vector.memset(w_nat[:].bitcast(I32), 0)
+        nc.vector.memset(ww_nat[:].bitcast(I32), 0)
         nc.vector.memset(wb_s[:].bitcast(I32), 0)
 
         cq_rows = cq.rearrange("(p t) c -> t p c", t=PACK)
         nc.scalar.dma_start(xo_stage[:], staged_rows(xo_scales))
-        nc.scalar.dma_start(w2_stage[:], staged_rows(w2_scales))
-        nc.sync.dma_start(xo_w[:].bitcast(I32), xo_words[0].rearrange("p n t -> p (n t)").bitcast(I32))
-        load_list("offs2", offs2)
-        nc.sync.dma_start(w2_raw[:].bitcast(I32), w2_words[0].bitcast(I32))
-        load_list("offs", offs)
         nc.sync.dma_start(cq_t[0][:], cq_rows[0])
+        load_list("offs", offs)
+        nc.scalar.dma_start(ga_sb[:], per_row(ga))
+        nc.sync.dma_start(ww_stage[:, 0], staged_rows(w_scales))
+        nc.sync.dma_start(ww_stage[:, 1], staged_rows(w2_scales))
         nc.sync.dma_start(cq_t[1][:], cq_rows[1])
-        load_list("offs4", offs4)
-        nc.sync.dma_start(w_stage[:], staged_rows(w_scales))
-        for t in range(2, PACK):
-            nc.sync.dma_start(cq_t[t][:], cq_rows[t])
-        nc.sync.dma_start(w_raw[:].bitcast(I32), w_words[0].rearrange("p n t -> p (n t)").bitcast(I32))
+        nc.sync.dma_start(cq_t[2][:], cq_rows[2])
+        load_list("offs2", offs2)
+        nc.sync.dma_start(wb_stage[:], staged_rows(wb_scales))
+        nc.sync.dma_start(cq_t[3][:], cq_rows[3])
+        nc.sync.dma_start(w_raw[:].bitcast(I32), words(w_words))
+        nc.sync.dma_start(xo_w[:].bitcast(I32), words(xo_words))
+        nc.sync.dma_start(w2_raw[:].bitcast(I32), w2_words[0].bitcast(I32))
+        nc.sync.dma_start(sa_sb[:], per_row(sa))
         load_list("offs3", offs3)
+        nc.sync.dma_start(sb_sb[:], per_row(sb))
+        load_list("offs4", offs4)
+        nc.sync.dma_start(tz_t[0][:], tz[0:P, :])
         nc.sync.dma_start(wb_w[:].bitcast(I32), wb_words[0].bitcast(I32))
+        nc.sync.dma_start(tz_t[1][:], tz[P:2 * P, :])
         load_list("offs5", offs5)
-        for s in range(N // P):
-            nc.sync.dma_start(tz_t[s][:], tz[s * P:(s + 1) * P, :])
-
-        nc.gpsimd.dma_start(ga_sb[:], ga.rearrange("(p t) o -> p (t o)", t=PACK))
-        nc.gpsimd.dma_start(sb_sb[:], sb.rearrange("(p t) o -> p (t o)", t=PACK))
-        nc.gpsimd.dma_start(sa_sb[:], sa.rearrange("(p t) o -> p (t o)", t=PACK))
         with nc.allow_non_contiguous_dma(reason="two steps a partition"):
-            nc.gpsimd.dma_start(so_sb[:], so.rearrange("(s p) o -> p (s o)", p=P))
-        nc.gpsimd.dma_start(wb_stage[:], staged_rows(wb_scales))
+            nc.sync.dma_start(so_sb[:], so.rearrange("(s p) o -> p (s o)", p=P))
 
         def spread_low(plane, stage):
             for q in range(QUADS):
@@ -112,52 +114,24 @@ def tile_list_weighedboth_codednote_one_stepfloor_kernel(
         def woven_in(ap):
             return ap.rearrange("p t (c i) -> p c t i", i=LINE)
 
-        banks = {}
-
         def bank(idx, width, name):
-            banks[name] = psum.tile([P, width], F32, name=name, tag=f"bank{idx}")
-            return banks[name]
+            return psum.tile([P, width], F32, name=name, tag=f"bank{idx}")
 
         spread_low(xo_s, xo_stage)
+        for q in range(QUADS):
+            nc.vector.tensor_copy(
+                ww_nat[:].bitcast(I32)[QUAD * q:QUAD * q + PACK, :].rearrange("p (w c) -> p w c", w=2),
+                ww_stage[:, :, q, :])
+        ww_s = sbuf("ww_s", [P, 2, PACK, P], U8)
+        nc.vector.tensor_copy(ww_s[:], ww_nat[:].rearrange("p (w m t) -> p w t m", w=2, t=PACK))
         xg_s = sbuf("xg_s", [P, J], U8)
         nc.vector.tensor_copy(xg_s[:], xo_s[:].indirect(lists["offs2"][:]))
-        xg_w = sbuf("xg_w", [P, J], U32)
-        nc.vector.tensor_copy(xg_w[:], xo_w[:].indirect(lists["offs2"][:]))
-        spread_low(w2_nat, w2_stage)
-        w2_s = sbuf("w2_s", [P, PACK, P], U8)
-        nc.vector.tensor_copy(w2_s[:], w2_nat[:].rearrange("p (m t) -> p t m", t=PACK))
-        w2_w = sbuf("w2_w", [P, PACK, 2 * P], U8)
-        nc.scalar.copy(dealt_out(w2_w[:].bitcast(U16)), dealt_in(w2_raw[:].bitcast(U16)))
 
-        x1 = sbuf("x1", [P, PACK, J], BF16)
-
-        def fetch_codes(t):
-            nc.scalar.activation(x1[:, t, :], cq_t[t][:].indirect(lists["offs"][:]), COPY, scale=ga_sb[:, t:t + 1])
-
-        b_t = [sbuf(f"b{t}", [P, J], F32) for t in range(PACK)]
-        gb = sbuf("gb", [P, PACK, O], F32)
-        for t in range(PACK):
-            acc = bank(t, J, f"bacc{t}")
-            nc.tensor.matmul_mx(acc[:], lhsT=w2_w[:, t, :].bitcast(E2M1), lhsT_scale=w2_s[:, t, :],
-                                rhs=xg_w[:].bitcast(E4M3), rhs_scale=xg_s[:], start=True, stop=True)
-            nc.vector.tensor_copy(b_t[t][:], acc[:])
-
-        spread_low(w_nat, w_stage)
-        w_s = sbuf("w_s", [P, PACK, P], U8)
-        nc.vector.tensor_copy(w_s[:], w_nat[:].rearrange("p (m t) -> p t m", t=PACK))
         spread_low(wb_s, wb_stage)
 
-        def fetch_b(t):
-            nc.scalar.activation(gb[:, t, :], b_t[t][:].indirect(lists["offs4"][:]), COPY, scale=sb_sb[:, t:t + 1])
-
-        fetch_codes(0)
-        fetch_codes(1)
-        fetch_b(0)
-        fetch_b(1)
-        fetch_codes(2)
-        fetch_b(2)
-        fetch_b(3)
-        fetch_codes(3)
+        x1 = sbuf("x1", [P, PACK, J], BF16)
+        for t in range(PACK):
+            nc.scalar.activation(x1[:, t, :], cq_t[t][:].indirect(lists["offs"][:]), COPY, scale=ga_sb[:, t:t + 1])
 
         w_w = sbuf("w_w", [P, PACK, P], U32)
         nc.scalar.copy(dealt_out(w_w[:]), dealt_in(w_raw[:]))
@@ -170,28 +144,46 @@ def tile_list_weighedboth_codednote_one_stepfloor_kernel(
         for h in halves:
             nc.vector.quantize_mx(out=xq_w[:, h].bitcast(E4M3), scales=xq_s[:, h],
                                   in_=x1i[:, h, :].rearrange("p j t -> p (j t)"))
+        xg_w = sbuf("xg_w", [P, J], U32)
+        nc.vector.tensor_copy(xg_w[:], xo_w[:].indirect(lists["offs2"][:]))
+        w2_w = sbuf("w2_w", [P, PACK, 2 * P], U8)
+        nc.scalar.copy(dealt_out(w2_w[:].bitcast(U16)), dealt_in(w2_raw[:].bitcast(U16)))
+
         a_t = [sbuf(f"a{t}", [P, J], F32) for t in range(PACK)]
         g_a = sbuf("g_a", [P, PACK, O], F32)
         for t in range(PACK):
-            acc = bank(PACK + t, J, f"aacc{t}")
-            nc.tensor.matmul_mx(acc[:], lhsT=w_w[:, t, :].bitcast(E4M3), lhsT_scale=w_s[:, t, :],
+            acc = bank(t, J, f"aacc{t}")
+            nc.tensor.matmul_mx(acc[:], lhsT=w_w[:, t, :].bitcast(E4M3), lhsT_scale=ww_s[:, 0, t, :],
                                 rhs=xq_w[:].bitcast(E4M3), rhs_scale=xq_s[:], start=True, stop=True)
             nc.vector.tensor_copy(a_t[t][:], acc[:])
             nc.scalar.activation(g_a[:, t, :], a_t[t][:].indirect(lists["offs3"][:]), COPY, scale=sa_sb[:, t:t + 1])
 
+        b_t = [sbuf(f"b{t}", [P, J], F32) for t in range(PACK)]
+        g_b = sbuf("g_b", [P, PACK, O], F32)
+        for t in range(PACK):
+            acc = bank(PACK + t, J, f"bacc{t}")
+            nc.tensor.matmul_mx(acc[:], lhsT=w2_w[:, t, :].bitcast(E2M1), lhsT_scale=ww_s[:, 1, t, :],
+                                rhs=xg_w[:].bitcast(E4M3), rhs_scale=xg_s[:], start=True, stop=True)
+            nc.vector.tensor_copy(b_t[t][:], acc[:])
+            nc.scalar.activation(g_b[:, t, :], b_t[t][:].indirect(lists["offs4"][:]), COPY, scale=sb_sb[:, t:t + 1])
+
         hid = sbuf("hid", [P, O, PACK], BF16)
-        nc.vector.tensor_tensor(woven_out(hid[:]), woven_in(g_a[:]), woven_in(gb[:]), MAX)
         hq_w = sbuf("hq_w", [P, O], U32)
         hq_s = sbuf("hq_s", [P, O], U8)
-        nc.vector.quantize_mx(out=hq_w[:].bitcast(E5M2), scales=hq_s[:], in_=hid[:].rearrange("p o t -> p (o t)"))
+        places = [slice(0, O // 2), slice(O // 2, O)]
+        for h in places:
+            nc.vector.tensor_tensor(woven_out(hid[:, h, :]), woven_in(g_a[:, :, h]), woven_in(g_b[:, :, h]), MAX)
+        for h in places:
+            nc.vector.quantize_mx(out=hq_w[:, h].bitcast(E5M2), scales=hq_s[:, h],
+                                  in_=hid[:, h, :].rearrange("p o t -> p (o t)"))
         queues = [nc.sync, nc.scalar]
+        floor = sbuf("floor", [P, N // P, O], F32, tag=f"b{PACK - 1}")
         for s in range(N // P):
-            floor = sbuf(f"floor{s}", [P, O], F32)
-            nc.scalar.activation(floor[:], tz_t[s][:].indirect(lists["offs5"][:]), COPY, scale=so_sb[:, s:s + 1])
+            nc.scalar.activation(floor[:, s, :], tz_t[s][:].indirect(lists["offs5"][:]), COPY, scale=so_sb[:, s:s + 1])
             acc = bank(s, O, f"pacc{s}")
             nc.tensor.matmul_mx(acc[:], lhsT=wb_w[:, 2 * P * s:2 * P * (s + 1)].bitcast(E2M1),
                                 lhsT_scale=wb_s[:, P * s:P * (s + 1)],
                                 rhs=hq_w[:].bitcast(E5M2), rhs_scale=hq_s[:], start=True, stop=True)
             y = sbuf(f"y{s}", [P, O], F32)
-            nc.vector.tensor_tensor(y[:], acc[:], floor[:], MAX)
+            nc.vector.tensor_tensor(y[:], acc[:], floor[:, s, :], MAX)
             queues[s].dma_start(out[s * P:(s + 1) * P, :], y[:])

@@ -98,6 +98,11 @@ def tile_list_weighedboth_codednote_one_stepfloor_kernel(
         with nc.allow_non_contiguous_dma(reason="two steps a partition"):
             nc.sync.dma_start(so_sb[:], so.rearrange("(s p) o -> p (s o)", p=P))
 
+        warm_in = sbuf("warm_in", [P, 1], F32)
+        warm_out = sbuf("warm_out", [P, 1], F32)
+        nc.gpsimd.memset(warm_in[:], 0.0)
+        nc.scalar.activation(warm_out[:], warm_in[:], COPY)
+
         def spread_low(plane, stage):
             for q in range(QUADS):
                 nc.vector.tensor_copy(plane[:].bitcast(I32)[QUAD * q:QUAD * q + PACK, :], stage[:, q, :])

from contextlib import ExitStack

import concourse.mybir as mybir

K, T, J, R, F, Z, O, N, E = 512, 1024, 256, 512, 512, 1024, 128, 256, 1024
FLOPS = 2 * (K * R * J + F * R * J + R * N * O)

F32 = mybir.dt.float32
BF16 = mybir.dt.bfloat16
I32 = mybir.dt.int32
U32 = mybir.dt.uint32
U16 = mybir.dt.uint16
U8 = mybir.dt.uint8
E4M3 = mybir.dt.float8_e4m3fn_x4
E5M2 = mybir.dt.float8_e5m2_x4
E2M1 = mybir.dt.float4_e2m1fn_x4
COPY = mybir.ActivationFunctionType.Copy
MAX = mybir.AluOpType.max

P = 128
PACK = 4
QUAD = 32
QUADS = P // QUAD
LINE = 4


def tile_list_weighedboth_codednote_one_stepfloor_kernel(
    tc, cq, ga, w_words, w_scales, xo_words, xo_scales, w2_words, w2_scales, sa, sb,
    wb_words, wb_scales, tz, so, offs, offs2, offs3, offs4, offs5, out,
):
    nc = tc.nc
    with ExitStack() as ctx:
        sb_pool = ctx.enter_context(tc.tile_pool(name="keep", bufs=1))
        psum = ctx.enter_context(tc.psum_pool(name="psum", bufs=1))

        def sbuf(name, shape, dtype, tag=None):
            return sb_pool.tile(shape, dtype, name=name, tag=tag or name, align_bytes=64)

        lists = {}

        def load_list(name, dram):
            lists[name] = sb_pool.tile(list(dram.shape), U16, name=name)
            nc.sync.dma_start(lists[name][:], dram)

        def staged_rows(scales):
            return scales[0].bitcast(I32).rearrange("(q r) c -> r q c", r=PACK)

        def per_row(v):
            return v.rearrange("(p t) o -> p (t o)", t=PACK)

        def words(v):
            return v[0].rearrange("p n t -> p (n t)").bitcast(I32)

        xo_w = sbuf("xo_w", [P, Z], U32)
        xo_stage = sbuf("xo_stage", [PACK, QUADS, Z // 4], I32)
        xo_s = sbuf("xo_s", [P, Z], U8)
        w2_raw = sbuf("w2_raw", [P, 2 * R], U8)
        w_raw = sbuf("w_raw", [P, R], U32)
        ww_stage = sbuf("ww_stage", [PACK, 2, QUADS, R // 4], I32)
        ww_nat = sbuf("ww_nat", [P, 2 * R], U8)
        wb_w = sbuf("wb_w", [P, 2 * N], U8)
        wb_stage = sbuf("wb_stage", [PACK, QUADS, N // 4], I32)
        wb_s = sbuf("wb_s", [P, N], U8)
        cq_t = [sbuf(f"cq{t}", [P, T], F32) for t in range(PACK)]
        tz_t = [sbuf(f"tz{s}", [P, E], F32) for s in range(N // P)]
        ga_sb = sbuf("ga_sb", [P, PACK], F32)
        sa_sb = sbuf("sa_sb", [P, PACK], F32)
        sb_sb = sbuf("sb_sb", [P, PACK], F32)
        so_sb = sbuf("so_sb", [P, N // P], F32)

        nc.vector.memset(xo_s[:].bitcast(I32), 0)
        nc.vector.memset(ww_nat[:].bitcast(I32), 0)
        nc.vector.memset(wb_s[:].bitcast(I32), 0)

        cq_rows = cq.rearrange("(p t) c -> t p c", t=PACK)
        nc.scalar.dma_start(xo_stage[:], staged_rows(xo_scales))
        nc.sync.dma_start(cq_t[0][:], cq_rows[0])
        load_list("offs", offs)
        nc.scalar.dma_start(ga_sb[:], per_row(ga))
        nc.sync.dma_start(ww_stage[:, 0], staged_rows(w_scales))
        nc.sync.dma_start(ww_stage[:, 1], staged_rows(w2_scales))
        nc.sync.dma_start(cq_t[1][:], cq_rows[1])
        nc.sync.dma_start(cq_t[2][:], cq_rows[2])
        load_list("offs2", offs2)
        nc.sync.dma_start(wb_stage[:], staged_rows(wb_scales))
        nc.sync.dma_start(cq_t[3][:], cq_rows[3])
        nc.sync.dma_start(w_raw[:].bitcast(I32), words(w_words))
        nc.sync.dma_start(xo_w[:].bitcast(I32), words(xo_words))
        nc.sync.dma_start(w2_raw[:].bitcast(I32), w2_words[0].bitcast(I32))
        nc.sync.dma_start(sa_sb[:], per_row(sa))
        load_list("offs3", offs3)
        nc.sync.dma_start(sb_sb[:], per_row(sb))
        load_list("offs4", offs4)
        nc.sync.dma_start(tz_t[0][:], tz[0:P, :])
        nc.sync.dma_start(wb_w[:].bitcast(I32), wb_words[0].bitcast(I32))
        nc.sync.dma_start(tz_t[1][:], tz[P:2 * P, :])
        load_list("offs5", offs5)
        with nc.allow_non_contiguous_dma(reason="two steps a partition"):
            nc.sync.dma_start(so_sb[:], so.rearrange("(s p) o -> p (s o)", p=P))

        warm_in = sbuf("warm_in", [P, 1], F32)
        warm_out = sbuf("warm_out", [P, 1], F32)
        nc.gpsimd.memset(warm_in[:], 0.0)
        nc.scalar.activation(warm_out[:], warm_in[:], COPY)

        def spread_low(plane, stage):
            for q in range(QUADS):
                nc.vector.tensor_copy(plane[:].bitcast(I32)[QUAD * q:QUAD * q + PACK, :], stage[:, q, :])

        def dealt_out(ap):
            return ap.rearrange("p t (c i) -> p c t i", i=LINE)

        def dealt_in(ap):
            return ap.rearrange("p (c i t) -> p c t i", i=LINE, t=PACK)

        def woven_out(ap):
            return ap.rearrange("p (c i) t -> p c t i", i=LINE)

        def woven_in(ap):
            return ap.rearrange("p t (c i) -> p c t i", i=LINE)

        def bank(idx, width, name):
            return psum.tile([P, width], F32, name=name, tag=f"bank{idx}")

        spread_low(xo_s, xo_stage)
        for q in range(QUADS):
            nc.vector.tensor_copy(
                ww_nat[:].bitcast(I32)[QUAD * q:QUAD * q + PACK, :].rearrange("p (w c) -> p w c", w=2),
                ww_stage[:, :, q, :])
        ww_s = sbuf("ww_s", [P, 2, PACK, P], U8)
        nc.vector.tensor_copy(ww_s[:], ww_nat[:].rearrange("p (w m t) -> p w t m", w=2, t=PACK))
        xg_s = sbuf("xg_s", [P, J], U8)
        nc.vector.tensor_copy(xg_s[:], xo_s[:].indirect(lists["offs2"][:]))

        spread_low(wb_s, wb_stage)

        x1 = sbuf("x1", [P, PACK, J], BF16)
        for t in range(PACK):
            nc.scalar.activation(x1[:, t, :], cq_t[t][:].indirect(lists["offs"][:]), COPY, scale=ga_sb[:, t:t + 1])

        w_w = sbuf("w_w", [P, PACK, P], U32)
        nc.scalar.copy(dealt_out(w_w[:]), dealt_in(w_raw[:]))
        x1i = sbuf("x1i", [P, J, PACK], BF16)
        xq_w = sbuf("xq_w", [P, J], U32)
        xq_s = sbuf("xq_s", [P, J], U8)
        halves = [slice(0, J // 2), slice(J // 2, J)]
        for h in halves:
            nc.vector.tensor_copy(woven_out(x1i[:, h, :]), woven_in(x1[:, :, h]))
        for h in halves:
            nc.vector.quantize_mx(out=xq_w[:, h].bitcast(E4M3), scales=xq_s[:, h],
                                  in_=x1i[:, h, :].rearrange("p j t -> p (j t)"))
        xg_w = sbuf("xg_w", [P, J], U32)
        nc.vector.tensor_copy(xg_w[:], xo_w[:].indirect(lists["offs2"][:]))
        w2_w = sbuf("w2_w", [P, PACK, 2 * P], U8)
        nc.scalar.copy(dealt_out(w2_w[:].bitcast(U16)), dealt_in(w2_raw[:].bitcast(U16)))

        a_t = [sbuf(f"a{t}", [P, J], F32) for t in range(PACK)]
        g_a = sbuf("g_a", [P, PACK, O], F32)
        for t in range(PACK):
            acc = bank(t, J, f"aacc{t}")
            nc.tensor.matmul_mx(acc[:], lhsT=w_w[:, t, :].bitcast(E4M3), lhsT_scale=ww_s[:, 0, t, :],
                                rhs=xq_w[:].bitcast(E4M3), rhs_scale=xq_s[:], start=True, stop=True)
            nc.vector.tensor_copy(a_t[t][:], acc[:])
            nc.scalar.activation(g_a[:, t, :], a_t[t][:].indirect(lists["offs3"][:]), COPY, scale=sa_sb[:, t:t + 1])

        b_t = [sbuf(f"b{t}", [P, J], F32) for t in range(PACK)]
        g_b = sbuf("g_b", [P, PACK, O], F32)
        for t in range(PACK):
            acc = bank(PACK + t, J, f"bacc{t}")
            nc.tensor.matmul_mx(acc[:], lhsT=w2_w[:, t, :].bitcast(E2M1), lhsT_scale=ww_s[:, 1, t, :],
                                rhs=xg_w[:].bitcast(E4M3), rhs_scale=xg_s[:], start=True, stop=True)
            nc.vector.tensor_copy(b_t[t][:], acc[:])
            nc.scalar.activation(g_b[:, t, :], b_t[t][:].indirect(lists["offs4"][:]), COPY, scale=sb_sb[:, t:t + 1])

        hid = sbuf("hid", [P, O, PACK], BF16)
        hq_w = sbuf("hq_w", [P, O], U32)
        hq_s = sbuf("hq_s", [P, O], U8)
        places = [slice(0, O // 2), slice(O // 2, O)]
        for h in places:
            nc.vector.tensor_tensor(woven_out(hid[:, h, :]), woven_in(g_a[:, :, h]), woven_in(g_b[:, :, h]), MAX)
        for h in places:
            nc.vector.quantize_mx(out=hq_w[:, h].bitcast(E5M2), scales=hq_s[:, h],
                                  in_=hid[:, h, :].rearrange("p o t -> p (o t)"))
        queues = [nc.sync, nc.scalar]
        floor = sbuf("floor", [P, N // P, O], F32, tag=f"b{PACK - 1}")
        for s in range(N // P):
            nc.scalar.activation(floor[:, s, :], tz_t[s][:].indirect(lists["offs5"][:]), COPY, scale=so_sb[:, s:s + 1])
            acc = bank(s, O, f"pacc{s}")
            nc.tensor.matmul_mx(acc[:], lhsT=wb_w[:, 2 * P * s:2 * P * (s + 1)].bitcast(E2M1),
                                lhsT_scale=wb_s[:, P * s:P * (s + 1)],
                                rhs=hq_w[:].bitcast(E5M2), rhs_scale=hq_s[:], start=True, stop=True)
            y = sbuf(f"y{s}", [P, O], F32)
            nc.vector.tensor_tensor(y[:], acc[:], floor[:, s, :], MAX)
            queues[s].dma_start(out[s * P:(s + 1) * P, :], y[:])
